import numpy as np
import ml_dtypes


def mxq(x, axis, fmt="e4m3"):
    dtype, down = {"e4m3": (ml_dtypes.float8_e4m3fn, 7), "e5m2": (ml_dtypes.float8_e5m2, 14)}[fmt]
    v = np.moveaxis(np.asarray(x, np.float32).astype(ml_dtypes.bfloat16).astype(np.float64), axis, -1)
    blocks = v.reshape(v.shape[:-1] + (-1, 32))
    amax = np.abs(blocks).max(-1, keepdims=True)
    byte = np.maximum(np.where(amax > 0, np.frexp(amax)[1] - 1 + 127, 0) - down, 1)
    scale = np.exp2(byte - 127.0)
    codes = (blocks / scale).astype(np.float32).astype(dtype).astype(np.float64)
    return np.moveaxis((codes * scale).reshape(v.shape), -1, axis)


WIDE = False


def mx_kscale(k):
    if not WIDE:
        return np.ones(k)
    levels = np.array([10, -10, 5, -5, 0])
    if k % 512:
        return np.exp2(np.random.permutation(np.resize(levels, k // 32))).repeat(32)
    a = np.empty((k // 512, 16))
    for p in range(k // 512):
        a[p, :8] = np.random.permutation(np.resize(levels, 8))
        for g in range(8):
            far = levels[np.abs(levels - a[p, g]) >= 10]
            a[p, g + 8] = far[np.random.randint(len(far))]
    return np.exp2(a.ravel()).repeat(32)


def f64(x):
    return np.asarray(x).astype(np.float64)


def striped(idx):
    return np.tile(idx.reshape(-1, 16).T, (8, 1)).astype(np.uint16)


def unstriped(offs):
    return offs[:16].T.reshape(-1).astype(np.int64)


def striped8(idx):
    return np.concatenate([x.reshape(-1, 16).T for x in idx]).astype(np.uint16)


def runs(offs, k):
    lists = np.stack([offs[16 * r : 16 * r + 16].T.reshape(-1) for r in range(8)]).astype(np.int64)
    return lists[np.arange(k) % 512 // 64]


def pack_weight(w):
    k, n = w.shape
    w = f64(np.asarray(w, np.float32).astype(ml_dtypes.bfloat16)).reshape(k // 32, 32, n)
    amax = np.abs(w).max(1)
    byte = np.clip(np.where(amax > 0, np.frexp(amax)[1] - 1 + 127 - 7, 1), 1, 254)
    scaled = (w * np.exp2(127.0 - byte)[:, None, :]).reshape(k, n).astype(np.float32)
    words = np.ascontiguousarray(scaled.reshape(k // 512, 128, 4, n).transpose(0, 1, 3, 2)).astype(ml_dtypes.float8_e4m3fn).view(np.uint8)
    return words, np.ascontiguousarray(byte.astype(np.uint8).reshape(k // 512, 16, n))


def unpack_weight(words, scales):
    g, p, n, _ = words.shape
    vals = np.ascontiguousarray(words).view(ml_dtypes.float8_e4m3fn).astype(np.float64) * np.repeat(np.exp2(scales.astype(np.float64) - 127.0), 8, axis=1)[..., None]
    return vals.transpose(0, 1, 3, 2).reshape(g * 512, n)


def sigmoid(v):
    return 1.0 / (1.0 + np.exp(-np.maximum(v, -700.0)))

def planes(y):
    n, m = y.shape
    v = y.astype(np.float32).astype(ml_dtypes.bfloat16).astype(np.float64).reshape(n // 32, 32, m)
    top = np.abs(v).max(1)
    byte = np.clip(np.where(top > 0, np.frexp(top)[1] - 1 + 127 - 7, 1), 1, 254)
    codes = (v * np.exp2(127.0 - byte)[:, None, :]).reshape(n, m).astype(np.float32).astype(ml_dtypes.float8_e4m3fn).view(np.uint8)
    words = codes.reshape(n // 512, 128, 4, m).transpose(0, 1, 3, 2)
    return np.ascontiguousarray(words), np.ascontiguousarray(byte.astype(np.uint8).reshape(n // 512, 16, m))


K, T, S, N, H = 512, 2048, 512, 512, 512


def setup_inputs():
    n = np.random.standard_normal
    s = mx_kscale(K)[:, None]
    u = mx_kscale(H)
    packed_xT = pack_weight(n((K, T)) * s)
    packed_w1 = pack_weight(n((K, H)) / np.sqrt(K) / s)
    packed_w2 = pack_weight(n((K, H)) / np.sqrt(K) / s)
    packed_w3 = pack_weight(n((K, H)) / np.sqrt(K) / s)
    packed_w4 = pack_weight(n((H, N)) / np.sqrt(H) / u[:, None])
    return {
        "x_words": packed_xT[0],
        "x_scales": packed_xT[1],
        "w1_words": packed_w1[0],
        "w1_scales": packed_w1[1],
        "w2_words": packed_w2[0],
        "w2_scales": packed_w2[1],
        "w3_words": packed_w3[0],
        "w3_scales": packed_w3[1],
        "gn": (np.random.uniform(0.5, 1.5, (H, 1)) * u[:, None]).astype(np.float32),
        "w4_words": packed_w4[0],
        "w4_scales": packed_w4[1],
        "offs": striped(np.random.permutation(T)[:S]),
        "two": striped(np.random.permutation(T)[:S]),
        "thr": striped(np.random.permutation(T)[:S]),
        "k0": striped8(np.stack([np.random.permutation(S) for _ in range(8)])),
        "k1": striped8(np.stack([np.random.permutation(S) for _ in range(8)])),
    }


def reference(x_words, x_scales, w1_words, w1_scales, w2_words, w2_scales, w3_words, w3_scales, gn, w4_words, w4_scales, offs, two, thr, k0, k1):
    xq = unpack_weight(x_words, x_scales)[:, unstriped(offs)]
    y = unpack_weight(w1_words, w1_scales).T @ xq
    a = y[np.arange(H)[:, None], runs(k0, H)]
    x_thr = unpack_weight(x_words, x_scales)[:, unstriped(thr)]
    d = sigmoid(unpack_weight(w3_words, w3_scales).T @ x_thr)
    tq = (d) ** 2
    sm = tq * (-2.0 * d + 3.0)
    b = y[np.arange(H)[:, None], runs(k1, H)]
    u1 = d * ((-1.0 * d + 1) ** 2)
    x_two = unpack_weight(x_words, x_scales)[:, unstriped(two)]
    c = unpack_weight(w2_words, w2_scales).T @ x_two
    w = tq * (d + -1.0)
    z = f64(gn) * (a + sm * (b - a) + u1 * (c[np.arange(H)[:, None], runs(k0, H)]) + w * (c[np.arange(H)[:, None], runs(k1, H)]))
    out_0 = unpack_weight(w4_words, w4_scales).T @ mxq(z, 0, "e4m3")
    return (out_0,) + planes(out_0)

@@ -1,0 +1,232 @@
+from contextlib import ExitStack
+
+import concourse.mybir as mybir
+from concourse.masks import make_identity
+
+K, T, S, N, H = 512, 2048, 512, 512, 512
+FLOPS = 2 * (3 * K * H * S + H * N * S)
+
+F32 = mybir.dt.float32
+BF16 = mybir.dt.bfloat16
+I32 = mybir.dt.int32
+U32 = mybir.dt.uint32
+U16 = mybir.dt.uint16
+U8 = mybir.dt.uint8
+FP8X4 = mybir.dt.float8_e4m3fn_x4
+ACT = mybir.ActivationFunctionType
+ALU = mybir.AluOpType
+
+P = 128
+PACK = 4
+QUADS = 4
+BLK = 128
+PIECES = ((0, 256), (256, 384), (384, 512))
+
+
+def tile_picked_hermite2_none_po_kernel(
+    tc, x_words, x_scales, w1_words, w1_scales, w2_words, w2_scales, w3_words, w3_scales, gn,
+    w4_words, w4_scales, offs, two, thr, k0, k1, out_0, out_1, out_2,
+):
+    nc = tc.nc
+    with ExitStack() as ctx:
+        keep = ctx.enter_context(tc.tile_pool(name="keep", bufs=1))
+        ring = ctx.enter_context(tc.tile_pool(name="ring", bufs=2))
+        psum = ctx.enter_context(tc.psum_pool(name="psum", bufs=1))
+
+        def load_list(name, src):
+            tile = keep.tile([P, S // 16], U16, name=name)
+            nc.sync.dma_start(tile[:], src)
+            return tile
+
+        def load_words(name, src, width):
+            tile = keep.tile([P, width], I32, name=name, align_bytes=64)
+            nc.sync.dma_start(tile[:], src[0].rearrange("p n t -> p (n t)").bitcast(I32))
+            return tile
+
+        def load_scale_rows(queue, tile, src, row):
+            for q in range(QUADS):
+                queue.dma_start(
+                    tile[32 * q + row : 32 * q + row + 4, :].bitcast(I32),
+                    src[0, 4 * q : 4 * q + 4, :].bitcast(I32),
+                )
+
+        def zeroed_bytes(name, width):
+            tile = keep.tile([P, width], U8, name=name, align_bytes=64)
+            nc.vector.memset(tile[:].bitcast(I32), 0)
+            return tile
+
+        def deal(name, tile, dtype):
+            dealt = keep.tile([P, H], dtype, name=name, align_bytes=64)
+            nc.vector.tensor_copy(
+                out=dealt[:].rearrange("p (t m) -> p m t", t=PACK),
+                in_=tile[:].rearrange("p (m t) -> p m t", t=PACK),
+            )
+            return dealt
+
+        xs = zeroed_bytes("xs", T)
+        s31 = zeroed_bytes("s31", H)
+        s24 = zeroed_bytes("s24", H)
+
+        thr_l = load_list("thr_l", thr)
+        xw = load_words("xw", x_words, T)
+        load_scale_rows(nc.sync, xs, x_scales, 0)
+        offs_l = load_list("offs_l", offs)
+        w3 = load_words("w3", w3_words, H)
+        w1 = load_words("w1", w1_words, H)
+        load_scale_rows(nc.sync, s31, w3_scales, 0)
+        load_scale_rows(nc.sync, s31, w1_scales, 4)
+        load_scale_rows(nc.gpsimd, s24, w2_scales, 0)
+        load_scale_rows(nc.gpsimd, s24, w4_scales, 4)
+        w2 = load_words("w2", w2_words, H)
+        two_l = load_list("two_l", two)
+        gain = keep.tile([P, PACK], F32, name="gain")
+        nc.sync.dma_start(gain[:], gn.rearrange("(p t) o -> p (t o)", t=PACK))
+        k1_l = load_list("k1_l", k1)
+        k0_l = load_list("k0_l", k0)
+        w4 = load_words("w4", w4_words, N)
+        ident = keep.tile([P, P], F32, name="ident")
+        make_identity(nc, ident[:])
+
+        def pick(name, lst):
+            words = keep.tile([P, S], U32, name=name + "_w", align_bytes=64)
+            nc.vector.tensor_copy(words[:], xw[:].bitcast(U32).indirect(lst[:]))
+            scales = keep.tile([P, S], U8, name=name + "_s", align_bytes=64)
+            nc.vector.tensor_copy(scales[:], xs[:].indirect(lst[:]))
+            return words, scales
+
+        def project(t, wd, sd, row, picked):
+            bank = psum.tile([P, S], F32, name="mm", tag="mm", bufs=3)
+            cols = slice(t * P, (t + 1) * P)
+            nc.tensor.matmul_mx(
+                out=bank[:], lhsT=wd[:, cols].bitcast(FP8X4), lhsT_scale=sd[row:P, cols],
+                rhs=picked[0][:].bitcast(FP8X4), rhs_scale=picked[1][:], start=True, stop=True,
+            )
+            return bank
+
+        x_thr = pick("x_thr", thr_l)
+        w3d = deal("w3d", w3, I32)
+        s31d = deal("s31d", s31, U8)
+        d, d2, e2 = [], [], []
+        for t in range(PACK):
+            bank = project(t, w3d, s31d, 0, x_thr)
+            d.append(keep.tile([P, S], F32, name="d%d" % t))
+            d2.append(keep.tile([P, S], F32, name="d2_%d" % t))
+            e2.append(keep.tile([P, S], F32, name="e2_%d" % t))
+            nc.scalar.activation(out=d[t][:], in_=bank[:], func=ACT.Sigmoid)
+            if t == 0:
+                nc.scalar.activation(out=d2[t][:], in_=d[t][:], func=ACT.Square)
+                nc.scalar.activation(out=e2[t][:], in_=d[t][:], func=ACT.Square, scale=-1.0, bias=1.0)
+
+        x_offs = pick("x_offs", offs_l)
+        w1d = deal("w1d", w1, I32)
+        x_two = pick("x_two", two_l)
+        w2d = deal("w2d", w2, I32)
+        s24d = deal("s24d", s24, U8)
+
+        z_scales = keep.tile([P, S], U8, name="z_scales", align_bytes=64)
+        z_codes = keep.tile([P, S], U32, name="z_codes", align_bytes=64)
+        o_scales = keep.tile([P, S], U8, name="o_scales", align_bytes=64)
+        o_codes = keep.tile([P, S], I32, name="o_codes", align_bytes=64)
+        y, c, h00, sm, u1, w = [], [], [], [], [], []
+
+        def windows(t):
+            for lst, wd, sd, row, picked, name in ((y, w1d, s31d, 4, x_offs, "y"), (c, w2d, s24d, 0, x_two, "c")):
+                bank = project(t, wd, sd, row, picked)
+                lst.append(keep.tile([P, S], F32, name="%s%d" % (name, t)))
+                nc.scalar.activation(out=lst[t][:], in_=bank[:], func=ACT.Copy, scale=gain[:, t : t + 1])
+
+        def coefficients(t):
+            if t > 0:
+                nc.scalar.activation(out=d2[t][:], in_=d[t][:], func=ACT.Square)
+                nc.scalar.activation(out=e2[t][:], in_=d[t][:], func=ACT.Square, scale=-1.0, bias=1.0)
+            for lst, name in ((h00, "h00_"), (sm, "sm"), (u1, "u1_"), (w, "w_")):
+                lst.append(keep.tile([P, S], F32, name="%s%d" % (name, t)))
+            nc.vector.scalar_tensor_tensor(out=w[t][:], in0=d[t][:], scalar=-1.0, in1=d2[t][:], op0=ALU.add, op1=ALU.mult)
+            nc.vector.tensor_tensor(out=u1[t][:], in0=d[t][:], in1=e2[t][:], op=ALU.mult)
+            nc.vector.scalar_tensor_tensor(out=sm[t][:], in0=w[t][:], scalar=-2.0, in1=d2[t][:], op0=ALU.mult, op1=ALU.add)
+            nc.scalar.activation(out=h00[t][:], in_=sm[t][:], func=ACT.Identity, scale=-1.0, bias=1.0)
+
+        def terms(lo, hi, t, zt):
+            entries = slice(lo // 16, hi // 16)
+            looked = ((y[t], k1_l, sm[t]), (c[t], k0_l, u1[t]), (c[t], k1_l, w[t]), (y[t], k0_l, h00[t]))
+            for q, (window, lst, coef) in enumerate(looked):
+                term = ring.tile([P, hi - lo], F32, name="term", tag="term", bufs=6)
+                nc.vector.tensor_tensor(term[:], window[:].indirect(lst[:, entries]), coef[:, lo:hi], ALU.mult)
+                for b in range((hi - lo) // BLK):
+                    nc.tensor.matmul(
+                        out=zt[b][:, t % 2, :], lhsT=term[:, b * BLK : (b + 1) * BLK], rhs=ident[:],
+                        is_transpose=True, start=(q == 0), stop=(q == len(looked) - 1),
+                    )
+
+        def turn_back(u, zt, back):
+            pairs = ring.tile([P, P, 2], BF16, name="pairs", tag="pairs", bufs=3)
+            nc.scalar.copy(out=pairs[:], in_=zt[:].rearrange("j e p -> j p e"))
+            nc.tensor.transpose(back[:, u, :], pairs[:].rearrange("j p e -> j (p e)").bitcast(F32), ident[:])
+
+        def quantize_z(j0, back):
+            grouped = ring.tile([P, BLK * PACK], BF16, name="grouped", tag="grouped", bufs=2, align_bytes=64)
+            nc.scalar.copy(
+                out=grouped[:].bitcast(F32).rearrange("p (j u) -> p j u", u=2), in_=back[:].rearrange("p u j -> p j u")
+            )
+            cols = slice(j0, j0 + BLK)
+            nc.vector.quantize_mx(out=z_codes[:, cols].bitcast(FP8X4), scales=z_scales[:, cols], in_=grouped[:])
+
+        def layer(j0, last):
+            cols = slice(j0, j0 + BLK)
+            bank = psum.tile([P, PACK, BLK], F32, name="mm", tag="mm", bufs=3)
+            for t in range(PACK):
+                rows = slice(t * P, (t + 1) * P)
+                nc.tensor.matmul_mx(
+                    out=bank[:, t, :], lhsT=w4d[:, rows].bitcast(FP8X4), lhsT_scale=s24d[4:P, rows],
+                    rhs=z_codes[:, cols].bitcast(FP8X4), rhs_scale=z_scales[:, cols], start=True, stop=True,
+                )
+            rounded = ring.tile([P, BLK * PACK], BF16, name="rounded", tag="rounded", bufs=2, align_bytes=64)
+            view_out = rounded[:].rearrange("p (j t) -> p j t", t=PACK)
+            view_in = bank[:].rearrange("p t j -> p j t")
+            if last:
+                nc.vector.tensor_copy(out=view_out, in_=view_in)
+            else:
+                nc.scalar.copy(out=view_out, in_=view_in)
+            result = ring.tile([P, PACK, BLK], F32, name="result", tag="result", bufs=4)
+            nc.scalar.copy(out=result[:], in_=bank[:])
+            nc.sync.dma_start(out_0.rearrange("(p t) j -> p t j", t=PACK)[:, :, cols], result[:])
+            return rounded
+
+        def quantize_out(j0, rounded):
+            cols = slice(j0, j0 + BLK)
+            nc.vector.quantize_mx(out=o_codes[:, cols].bitcast(FP8X4), scales=o_scales[:, cols], in_=rounded[:])
+            nc.sync.dma_start(out_1[0].rearrange("p n t -> p (n t)").bitcast(I32)[:, cols], o_codes[:, cols])
+
+        pending = []
+        for lo, hi in PIECES:
+            blocks = range(lo, hi, BLK)
+            back = [psum.tile([P, 2, BLK], F32, name="back", tag="back", bufs=2) for j0 in blocks]
+            for t in range(PACK):
+                if lo == 0:
+                    coefficients(t)
+                    windows(t)
+                    if t == 1:
+                        w4d = deal("w4d", w4, I32)
+                if t % 2 == 0:
+                    zt = [psum.tile([P, 2, P], F32, name="zt", tag="zt", bufs=3) for j0 in blocks]
+                terms(lo, hi, t, zt)
+                if t == 0:
+                    for j0, old in pending:
+                        quantize_z(j0, old)
+                if t == 1:
+                    pending = [(j0, layer(j0, False)) for j0, old in pending]
+                if t == 2:
+                    for j0, rounded in pending:
+                        quantize_out(j0, rounded)
+                if t % 2 == 1:
+                    for b in range(len(blocks)):
+                        turn_back(t // 2, zt[b], back[b])
+            pending = list(zip(blocks, back))
+        for j0, old in pending:
+            quantize_z(j0, old)
+            quantize_out(j0, layer(j0, True))
+        for q in range(QUADS):
+            queue = nc.scalar if q % 2 else nc.sync
+            queue.dma_start(
+                out_2[0, 4 * q : 4 * q + 4, :].bitcast(I32), o_scales[32 * q : 32 * q + 4, :].bitcast(I32)
+            )

@@ -43,56 +43,57 @@ def tile_picked_hermite2_none_po_kernel(
             nc.sync.dma_start(tile[:], src[0].rearrange("p n t -> p (n t)").bitcast(I32))
             return tile
 
-        def load_scale_rows(queue, tile, src, row):
-            for q in range(QUADS):
+        def load_scale_rows(queue, tile, src, slot, slots):
+            width = src.shape[2] // 4
+            rows = src[0].bitcast(I32).rearrange("(q r) w -> r q w", r=4)
+            for r in range(4):
                 queue.dma_start(
-                    tile[32 * q + row : 32 * q + row + 4, :].bitcast(I32),
-                    src[0, 4 * q : 4 * q + 4, :].bitcast(I32),
+                    tile[4 * slot + r : P : 4 * slots, :].bitcast(I32),
+                    rows[r].unsqueeze(1).to_broadcast([QUADS, 8 // slots, width]),
                 )
-
-        def zeroed_bytes(name, width):
-            tile = keep.tile([P, width], U8, name=name, align_bytes=64)
-            nc.vector.memset(tile[:].bitcast(I32), 0)
-            return tile
 
         def deal(name, tile, dtype):
             dealt = keep.tile([P, H], dtype, name=name, align_bytes=64)
-            nc.vector.tensor_copy(
-                out=dealt[:].rearrange("p (t m) -> p m t", t=PACK),
-                in_=tile[:].rearrange("p (m t) -> p m t", t=PACK),
+            nc.gpsimd.tensor_copy(
+                out=dealt[:].rearrange("p (t m) -> p t m", t=PACK),
+                in_=tile[:].rearrange("p (m t) -> p t m", t=PACK),
             )
             return dealt
 
-        xs = zeroed_bytes("xs", T)
-        s31 = zeroed_bytes("s31", H)
-        s24 = zeroed_bytes("s24", H)
-
+        s31 = keep.tile([P, H], U8, name="s31", align_bytes=64)
+        s24 = keep.tile([P, H], U8, name="s24", align_bytes=64)
         thr_l = load_list("thr_l", thr)
-        xw = load_words("xw", x_words, T)
-        load_scale_rows(nc.sync, xs, x_scales, 0)
+        xs = keep.tile([P, T], U8, name="xs", align_bytes=64)
+        for q in range(QUADS):
+            rows = x_scales[0, 4 * q : 4 * q + 4, :].bitcast(I32)
+            nc.sync.dma_start(xs[32 * q : 32 * q + 32, :].bitcast(I32), rows.unsqueeze(0).to_broadcast([8, 4, T // 4]))
         offs_l = load_list("offs_l", offs)
-        w3 = load_words("w3", w3_words, H)
-        w1 = load_words("w1", w1_words, H)
-        load_scale_rows(nc.sync, s31, w3_scales, 0)
-        load_scale_rows(nc.sync, s31, w1_scales, 4)
-        load_scale_rows(nc.gpsimd, s24, w2_scales, 0)
-        load_scale_rows(nc.gpsimd, s24, w4_scales, 4)
-        w2 = load_words("w2", w2_words, H)
         two_l = load_list("two_l", two)
+        xw = load_words("xw", x_words, T)
+        w3 = load_words("w3", w3_words, H)
+        load_scale_rows(nc.sync, s31, w3_scales, 0, 2)
+        load_scale_rows(nc.gpsimd, s31, w1_scales, 1, 2)
         gain = keep.tile([P, PACK], F32, name="gain")
-        nc.sync.dma_start(gain[:], gn.rearrange("(p t) o -> p (t o)", t=PACK))
+        nc.gpsimd.dma_start(gain[:], gn.rearrange("(p t) o -> p (t o)", t=PACK))
+        w1 = load_words("w1", w1_words, H)
+        w2 = load_words("w2", w2_words, H)
+        w4 = load_words("w4", w4_words, N)
+        load_scale_rows(nc.sync, s24, w2_scales, 0, 2)
+        load_scale_rows(nc.sync, s24, w4_scales, 1, 2)
         k1_l = load_list("k1_l", k1)
         k0_l = load_list("k0_l", k0)
-        w4 = load_words("w4", w4_words, N)
         ident = keep.tile([P, P], F32, name="ident")
         make_identity(nc, ident[:])
 
-        def pick(name, lst):
-            words = keep.tile([P, S], U32, name=name + "_w", align_bytes=64)
+        def pick_words(name, lst):
+            words = keep.tile([P, S], U32, name=name, align_bytes=64)
             nc.vector.tensor_copy(words[:], xw[:].bitcast(U32).indirect(lst[:]))
-            scales = keep.tile([P, S], U8, name=name + "_s", align_bytes=64)
+            return words
+
+        def pick_scales(name, lst):
+            scales = keep.tile([P, S], U8, name=name, align_bytes=64)
             nc.vector.tensor_copy(scales[:], xs[:].indirect(lst[:]))
-            return words, scales
+            return scales
 
         def project(t, wd, sd, row, picked):
             bank = psum.tile([P, S], F32, name="mm", tag="mm", bufs=3)
@@ -103,25 +104,27 @@ def tile_picked_hermite2_none_po_kernel(
             )
             return bank
 
-        x_thr = pick("x_thr", thr_l)
+        thr_s = pick_scales("thr_s", thr_l)
+        offs_s = pick_scales("offs_s", offs_l)
+        x_thr = (pick_words("thr_w", thr_l), thr_s)
+        two_s = pick_scales("two_s", two_l)
+        x_offs = (pick_words("offs_w", offs_l), offs_s)
+        x_two = (pick_words("two_w", two_l), two_s)
         w3d = deal("w3d", w3, I32)
         s31d = deal("s31d", s31, U8)
-        d, d2, e2 = [], [], []
-        for t in range(PACK):
-            bank = project(t, w3d, s31d, 0, x_thr)
-            d.append(keep.tile([P, S], F32, name="d%d" % t))
-            d2.append(keep.tile([P, S], F32, name="d2_%d" % t))
-            e2.append(keep.tile([P, S], F32, name="e2_%d" % t))
-            nc.scalar.activation(out=d[t][:], in_=bank[:], func=ACT.Sigmoid)
-            if t == 0:
-                nc.scalar.activation(out=d2[t][:], in_=d[t][:], func=ACT.Square)
-                nc.scalar.activation(out=e2[t][:], in_=d[t][:], func=ACT.Square, scale=-1.0, bias=1.0)
-
-        x_offs = pick("x_offs", offs_l)
         w1d = deal("w1d", w1, I32)
-        x_two = pick("x_two", two_l)
         w2d = deal("w2d", w2, I32)
         s24d = deal("s24d", s24, U8)
+        w4d = deal("w4d", w4, I32)
+        d, d2, e2 = [], [], []
+
+        def positions(t):
+            bank = project(t, w3d, s31d, 0, x_thr)
+            for lst, name in ((d, "d"), (d2, "d2_"), (e2, "e2_")):
+                lst.append(keep.tile([P, S], F32, name="%s%d" % (name, t)))
+            nc.scalar.activation(out=d[t][:], in_=bank[:], func=ACT.Sigmoid)
+            nc.scalar.activation(out=d2[t][:], in_=d[t][:], func=ACT.Square)
+            nc.scalar.activation(out=e2[t][:], in_=d[t][:], func=ACT.Square, scale=-1.0, bias=1.0)
 
         z_scales = keep.tile([P, S], U8, name="z_scales", align_bytes=64)
         z_codes = keep.tile([P, S], U32, name="z_codes", align_bytes=64)
@@ -136,9 +139,6 @@ def tile_picked_hermite2_none_po_kernel(
                 nc.scalar.activation(out=lst[t][:], in_=bank[:], func=ACT.Copy, scale=gain[:, t : t + 1])
 
         def coefficients(t):
-            if t > 0:
-                nc.scalar.activation(out=d2[t][:], in_=d[t][:], func=ACT.Square)
-                nc.scalar.activation(out=e2[t][:], in_=d[t][:], func=ACT.Square, scale=-1.0, bias=1.0)
             for lst, name in ((h00, "h00_"), (sm, "sm"), (u1, "u1_"), (w, "w_")):
                 lst.append(keep.tile([P, S], F32, name="%s%d" % (name, t)))
             nc.vector.scalar_tensor_tensor(out=w[t][:], in0=d[t][:], scalar=-1.0, in1=d2[t][:], op0=ALU.add, op1=ALU.mult)
@@ -203,10 +203,9 @@ def tile_picked_hermite2_none_po_kernel(
             back = [psum.tile([P, 2, BLK], F32, name="back", tag="back", bufs=2) for j0 in blocks]
             for t in range(PACK):
                 if lo == 0:
-                    coefficients(t)
+                    positions(t)
                     windows(t)
-                    if t == 1:
-                        w4d = deal("w4d", w4, I32)
+                    coefficients(t)
                 if t % 2 == 0:
                     zt = [psum.tile([P, 2, P], F32, name="zt", tag="zt", bufs=3) for j0 in blocks]
                 terms(lo, hi, t, zt)

@@ -39,7 +39,7 @@ def tile_picked_hermite2_none_po_kernel(
             return tile
 
         def load_words(name, src, width):
-            tile = keep.tile([P, width], I32, name=name, align_bytes=64)
+            tile = keep.tile([P, width], I32, name=name, tag=name, align_bytes=64)
             nc.sync.dma_start(tile[:], src[0].rearrange("p n t -> p (n t)").bitcast(I32))
             return tile
 
@@ -52,46 +52,48 @@ def tile_picked_hermite2_none_po_kernel(
                     rows[r].unsqueeze(1).to_broadcast([QUADS, 8 // slots, width]),
                 )
 
-        def deal(name, tile, dtype):
+        def deal(name, tile, dtype, run):
             dealt = keep.tile([P, H], dtype, name=name, align_bytes=64)
-            nc.gpsimd.tensor_copy(
-                out=dealt[:].rearrange("p (t m) -> p t m", t=PACK),
-                in_=tile[:].rearrange("p (m t) -> p t m", t=PACK),
+            nc.vector.tensor_copy(
+                out=dealt[:].rearrange("p (t c i) -> p c t i", t=PACK, i=run),
+                in_=tile[:].rearrange("p (c i t) -> p c t i", t=PACK, i=run),
             )
             return dealt
 
-        s31 = keep.tile([P, H], U8, name="s31", align_bytes=64)
-        s24 = keep.tile([P, H], U8, name="s24", align_bytes=64)
-        thr_l = load_list("thr_l", thr)
         xs = keep.tile([P, T], U8, name="xs", align_bytes=64)
+        s3 = keep.tile([P, H], U8, name="s3", tag="s3", align_bytes=64)
+        s12 = keep.tile([P, H], U8, name="s12", align_bytes=64)
+        s4 = keep.tile([P, N], U8, name="s4", align_bytes=64)
+
+        thr_l = load_list("thr_l", thr)
         for q in range(QUADS):
             rows = x_scales[0, 4 * q : 4 * q + 4, :].bitcast(I32)
             nc.sync.dma_start(xs[32 * q : 32 * q + 32, :].bitcast(I32), rows.unsqueeze(0).to_broadcast([8, 4, T // 4]))
         offs_l = load_list("offs_l", offs)
-        two_l = load_list("two_l", two)
         xw = load_words("xw", x_words, T)
         w3 = load_words("w3", w3_words, H)
-        load_scale_rows(nc.sync, s31, w3_scales, 0, 2)
-        load_scale_rows(nc.gpsimd, s31, w1_scales, 1, 2)
-        gain = keep.tile([P, PACK], F32, name="gain")
-        nc.gpsimd.dma_start(gain[:], gn.rearrange("(p t) o -> p (t o)", t=PACK))
+        load_scale_rows(nc.sync, s3, w3_scales, 0, 1)
+        two_l = load_list("two_l", two)
         w1 = load_words("w1", w1_words, H)
         w2 = load_words("w2", w2_words, H)
-        w4 = load_words("w4", w4_words, N)
-        load_scale_rows(nc.sync, s24, w2_scales, 0, 2)
-        load_scale_rows(nc.sync, s24, w4_scales, 1, 2)
+        gain = keep.tile([P, PACK], F32, name="gain")
+        nc.sync.dma_start(gain[:], gn.rearrange("(p t) o -> p (t o)", t=PACK))
+        load_scale_rows(nc.sync, s12, w1_scales, 0, 2)
+        load_scale_rows(nc.sync, s12, w2_scales, 1, 2)
         k1_l = load_list("k1_l", k1)
         k0_l = load_list("k0_l", k0)
+        w4 = load_words("w4", w4_words, N)
+        load_scale_rows(nc.sync, s4, w4_scales, 0, 1)
         ident = keep.tile([P, P], F32, name="ident")
         make_identity(nc, ident[:])
 
-        def pick_words(name, lst):
-            words = keep.tile([P, S], U32, name=name, align_bytes=64)
+        def pick_words(name, lst, slot):
+            words = keep.tile([P, S], U32, name=name, tag=slot, align_bytes=64)
             nc.vector.tensor_copy(words[:], xw[:].bitcast(U32).indirect(lst[:]))
             return words
 
-        def pick_scales(name, lst):
-            scales = keep.tile([P, S], U8, name=name, align_bytes=64)
+        def pick_scales(name, lst, slot):
+            scales = keep.tile([P, S], U8, name=name, tag=slot, align_bytes=64)
             nc.vector.tensor_copy(scales[:], xs[:].indirect(lst[:]))
             return scales
 
@@ -104,22 +106,23 @@ def tile_picked_hermite2_none_po_kernel(
             )
             return bank
 
-        thr_s = pick_scales("thr_s", thr_l)
-        offs_s = pick_scales("offs_s", offs_l)
-        x_thr = (pick_words("thr_w", thr_l), thr_s)
-        two_s = pick_scales("two_s", two_l)
-        x_offs = (pick_words("offs_w", offs_l), offs_s)
-        x_two = (pick_words("two_w", two_l), two_s)
-        w3d = deal("w3d", w3, I32)
-        s31d = deal("s31d", s31, U8)
-        w1d = deal("w1d", w1, I32)
-        w2d = deal("w2d", w2, I32)
-        s24d = deal("s24d", s24, U8)
-        w4d = deal("w4d", w4, I32)
+        thr_s = pick_scales("thr_s", thr_l, "thr_s")
+        offs_s = pick_scales("offs_s", offs_l, "offs_s")
+        x_thr = (pick_words("thr_w", thr_l, "thr_w"), thr_s)
+        w3d = deal("w3d", w3, I32, 4)
+        s3d = deal("s3d", s3, U8, 16)
+        two_s = pick_scales("two_s", two_l, "s3")
+        x_offs = (pick_words("offs_w", offs_l, "w3"), offs_s)
+        w1d = deal("w1d", w1, I32, 4)
+        s12d = deal("s12d", s12, U8, 16)
+        x_two = (pick_words("two_w", two_l, "w1"), two_s)
+        w2d = deal("w2d", w2, I32, 4)
+        w4d = deal("w4d", w4, I32, 4)
+        s4d = deal("s4d", s4, U8, 16)
         d, d2, e2 = [], [], []
 
         def positions(t):
-            bank = project(t, w3d, s31d, 0, x_thr)
+            bank = project(t, w3d, s3d, 0, x_thr)
             for lst, name in ((d, "d"), (d2, "d2_"), (e2, "e2_")):
                 lst.append(keep.tile([P, S], F32, name="%s%d" % (name, t)))
             nc.scalar.activation(out=d[t][:], in_=bank[:], func=ACT.Sigmoid)
@@ -133,7 +136,7 @@ def tile_picked_hermite2_none_po_kernel(
         y, c, h00, sm, u1, w = [], [], [], [], [], []
 
         def windows(t):
-            for lst, wd, sd, row, picked, name in ((y, w1d, s31d, 4, x_offs, "y"), (c, w2d, s24d, 0, x_two, "c")):
+            for lst, wd, sd, row, picked, name in ((y, w1d, s12d, 0, x_offs, "y"), (c, w2d, s12d, 4, x_two, "c")):
                 bank = project(t, wd, sd, row, picked)
                 lst.append(keep.tile([P, S], F32, name="%s%d" % (name, t)))
                 nc.scalar.activation(out=lst[t][:], in_=bank[:], func=ACT.Copy, scale=gain[:, t : t + 1])
@@ -150,7 +153,7 @@ def tile_picked_hermite2_none_po_kernel(
             entries = slice(lo // 16, hi // 16)
             looked = ((y[t], k1_l, sm[t]), (c[t], k0_l, u1[t]), (c[t], k1_l, w[t]), (y[t], k0_l, h00[t]))
             for q, (window, lst, coef) in enumerate(looked):
-                term = ring.tile([P, hi - lo], F32, name="term", tag="term", bufs=6)
+                term = ring.tile([P, hi - lo], F32, name="term", tag="term", bufs=12)
                 nc.vector.tensor_tensor(term[:], window[:].indirect(lst[:, entries]), coef[:, lo:hi], ALU.mult)
                 for b in range((hi - lo) // BLK):
                     nc.tensor.matmul(
@@ -171,25 +174,40 @@ def tile_picked_hermite2_none_po_kernel(
             cols = slice(j0, j0 + BLK)
             nc.vector.quantize_mx(out=z_codes[:, cols].bitcast(FP8X4), scales=z_scales[:, cols], in_=grouped[:])
 
-        def layer(j0, last):
+        def last_product(j0, t, out):
             cols = slice(j0, j0 + BLK)
+            rows = slice(t * P, (t + 1) * P)
+            nc.tensor.matmul_mx(
+                out=out, lhsT=w4d[:, rows].bitcast(FP8X4), lhsT_scale=s4d[:, rows],
+                rhs=z_codes[:, cols].bitcast(FP8X4), rhs_scale=z_scales[:, cols], start=True, stop=True,
+            )
+
+        out_rows = out_0.rearrange("(p t) j -> p t j", t=PACK)
+
+        def layer(j0):
             bank = psum.tile([P, PACK, BLK], F32, name="mm", tag="mm", bufs=3)
             for t in range(PACK):
-                rows = slice(t * P, (t + 1) * P)
-                nc.tensor.matmul_mx(
-                    out=bank[:, t, :], lhsT=w4d[:, rows].bitcast(FP8X4), lhsT_scale=s24d[4:P, rows],
-                    rhs=z_codes[:, cols].bitcast(FP8X4), rhs_scale=z_scales[:, cols], start=True, stop=True,
-                )
+                last_product(j0, t, bank[:, t, :])
             rounded = ring.tile([P, BLK * PACK], BF16, name="rounded", tag="rounded", bufs=2, align_bytes=64)
-            view_out = rounded[:].rearrange("p (j t) -> p j t", t=PACK)
-            view_in = bank[:].rearrange("p t j -> p j t")
-            if last:
-                nc.vector.tensor_copy(out=view_out, in_=view_in)
-            else:
-                nc.scalar.copy(out=view_out, in_=view_in)
+            nc.scalar.copy(out=rounded[:].rearrange("p (j t) -> p j t", t=PACK), in_=bank[:].rearrange("p t j -> p j t"))
             result = ring.tile([P, PACK, BLK], F32, name="result", tag="result", bufs=4)
             nc.scalar.copy(out=result[:], in_=bank[:])
-            nc.sync.dma_start(out_0.rearrange("(p t) j -> p t j", t=PACK)[:, :, cols], result[:])
+            nc.sync.dma_start(out_rows[:, :, j0 : j0 + BLK], result[:])
+            return rounded
+
+        def last_layer(j0):
+            result = ring.tile([P, PACK, BLK], F32, name="result", tag="result", bufs=4)
+            for u, copy in enumerate((nc.scalar.copy, nc.vector.tensor_copy)):
+                bank = psum.tile([P, 2, BLK], F32, name="mm", tag="mm", bufs=3)
+                for e in range(2):
+                    last_product(j0, 2 * u + e, bank[:, e, :])
+                copy(out=result[:, 2 * u : 2 * u + 2, :], in_=bank[:])
+            nc.scalar.dma_start(out_rows[:, :, j0 : j0 + BLK], result[:])
+            rounded = ring.tile([P, BLK * PACK], BF16, name="rounded", tag="rounded", bufs=2, align_bytes=64)
+            nc.vector.tensor_copy(
+                out=rounded[:].rearrange("p (c i t) -> p c t i", t=PACK, i=4),
+                in_=result[:].rearrange("p t (c i) -> p c t i", i=4),
+            )
             return rounded
 
         def quantize_out(j0, rounded):
@@ -213,7 +231,7 @@ def tile_picked_hermite2_none_po_kernel(
                     for j0, old in pending:
                         quantize_z(j0, old)
                 if t == 1:
-                    pending = [(j0, layer(j0, False)) for j0, old in pending]
+                    pending = [(j0, layer(j0)) for j0, old in pending]
                 if t == 2:
                     for j0, rounded in pending:
                         quantize_out(j0, rounded)
@@ -223,7 +241,7 @@ def tile_picked_hermite2_none_po_kernel(
             pending = list(zip(blocks, back))
         for j0, old in pending:
             quantize_z(j0, old)
-            quantize_out(j0, layer(j0, True))
+            quantize_out(j0, last_layer(j0))
         for q in range(QUADS):
             queue = nc.scalar if q % 2 else nc.sync
             queue.dma_start(

@@ -43,47 +43,47 @@ def tile_picked_hermite2_none_po_kernel(
             nc.sync.dma_start(tile[:], src[0].rearrange("p n t -> p (n t)").bitcast(I32))
             return tile
 
-        def load_scale_rows(queue, tile, src, slot, slots):
-            width = src.shape[2] // 4
-            rows = src[0].bitcast(I32).rearrange("(q r) w -> r q w", r=4)
-            for r in range(4):
+        def load_scale_rows(queue, tile, src, row):
+            for q in range(QUADS):
                 queue.dma_start(
-                    tile[4 * slot + r : P : 4 * slots, :].bitcast(I32),
-                    rows[r].unsqueeze(1).to_broadcast([QUADS, 8 // slots, width]),
+                    tile[32 * q + row : 32 * q + row + 4, :].bitcast(I32),
+                    src[0, 4 * q : 4 * q + 4, :].bitcast(I32),
                 )
 
-        def deal(name, tile, dtype, run):
-            dealt = keep.tile([P, H], dtype, name=name, align_bytes=64)
+        def zeroed_bytes(engine, name, width):
+            tile = keep.tile([P, width], U8, name=name, tag=name, align_bytes=64)
+            engine.memset(tile[:].bitcast(I32), 0)
+            return tile
+
+        def deal(name, tile, dtype, run, slot=None):
+            dealt = keep.tile([P, H], dtype, name=name, tag=slot or name, align_bytes=64)
             nc.vector.tensor_copy(
                 out=dealt[:].rearrange("p (t c i) -> p c t i", t=PACK, i=run),
                 in_=tile[:].rearrange("p (c i t) -> p c t i", t=PACK, i=run),
             )
             return dealt
 
-        xs = keep.tile([P, T], U8, name="xs", align_bytes=64)
-        s3 = keep.tile([P, H], U8, name="s3", tag="s3", align_bytes=64)
-        s12 = keep.tile([P, H], U8, name="s12", align_bytes=64)
-        s4 = keep.tile([P, N], U8, name="s4", align_bytes=64)
+        xs = zeroed_bytes(nc.vector, "xs", T)
+        s31 = zeroed_bytes(nc.vector, "s31", H)
+        s24 = zeroed_bytes(nc.gpsimd, "s24", H)
 
+        w3 = load_words("w3", w3_words, H)
+        load_scale_rows(nc.sync, xs, x_scales, 0)
         thr_l = load_list("thr_l", thr)
-        for q in range(QUADS):
-            rows = x_scales[0, 4 * q : 4 * q + 4, :].bitcast(I32)
-            nc.sync.dma_start(xs[32 * q : 32 * q + 32, :].bitcast(I32), rows.unsqueeze(0).to_broadcast([8, 4, T // 4]))
         offs_l = load_list("offs_l", offs)
         xw = load_words("xw", x_words, T)
-        w3 = load_words("w3", w3_words, H)
-        load_scale_rows(nc.sync, s3, w3_scales, 0, 1)
         two_l = load_list("two_l", two)
         w1 = load_words("w1", w1_words, H)
         w2 = load_words("w2", w2_words, H)
+        k0_l = load_list("k0_l", k0)
+        k1_l = load_list("k1_l", k1)
         gain = keep.tile([P, PACK], F32, name="gain")
         nc.sync.dma_start(gain[:], gn.rearrange("(p t) o -> p (t o)", t=PACK))
-        load_scale_rows(nc.sync, s12, w1_scales, 0, 2)
-        load_scale_rows(nc.sync, s12, w2_scales, 1, 2)
-        k1_l = load_list("k1_l", k1)
-        k0_l = load_list("k0_l", k0)
+        load_scale_rows(nc.sync, s31, w3_scales, 0)
+        load_scale_rows(nc.sync, s31, w1_scales, 4)
         w4 = load_words("w4", w4_words, N)
-        load_scale_rows(nc.sync, s4, w4_scales, 0, 1)
+        load_scale_rows(nc.gpsimd, s24, w2_scales, 0)
+        load_scale_rows(nc.gpsimd, s24, w4_scales, 4)
         ident = keep.tile([P, P], F32, name="ident")
         make_identity(nc, ident[:])
 
@@ -106,23 +106,22 @@ def tile_picked_hermite2_none_po_kernel(
             )
             return bank
 
+        w3d = deal("w3d", w3, I32, 4)
         thr_s = pick_scales("thr_s", thr_l, "thr_s")
         offs_s = pick_scales("offs_s", offs_l, "offs_s")
         x_thr = (pick_words("thr_w", thr_l, "thr_w"), thr_s)
-        w3d = deal("w3d", w3, I32, 4)
-        s3d = deal("s3d", s3, U8, 16)
-        two_s = pick_scales("two_s", two_l, "s3")
-        x_offs = (pick_words("offs_w", offs_l, "w3"), offs_s)
+        two_s = pick_scales("two_s", two_l, "two_s")
+        x_offs = (pick_words("offs_w", offs_l, "offs_w"), offs_s)
+        s31d = deal("s31d", s31, U8, 16)
+        x_two = (pick_words("two_w", two_l, "s31"), two_s)
         w1d = deal("w1d", w1, I32, 4)
-        s12d = deal("s12d", s12, U8, 16)
-        x_two = (pick_words("two_w", two_l, "w1"), two_s)
         w2d = deal("w2d", w2, I32, 4)
+        s24d = deal("s24d", s24, U8, 16, "xw")
         w4d = deal("w4d", w4, I32, 4)
-        s4d = deal("s4d", s4, U8, 16)
         d, d2, e2 = [], [], []
 
         def positions(t):
-            bank = project(t, w3d, s3d, 0, x_thr)
+            bank = project(t, w3d, s31d, 0, x_thr)
             for lst, name in ((d, "d"), (d2, "d2_"), (e2, "e2_")):
                 lst.append(keep.tile([P, S], F32, name="%s%d" % (name, t)))
             nc.scalar.activation(out=d[t][:], in_=bank[:], func=ACT.Sigmoid)
@@ -136,7 +135,7 @@ def tile_picked_hermite2_none_po_kernel(
         y, c, h00, sm, u1, w = [], [], [], [], [], []
 
         def windows(t):
-            for lst, wd, sd, row, picked, name in ((y, w1d, s12d, 0, x_offs, "y"), (c, w2d, s12d, 4, x_two, "c")):
+            for lst, wd, sd, row, picked, name in ((y, w1d, s31d, 4, x_offs, "y"), (c, w2d, s24d, 0, x_two, "c")):
                 bank = project(t, wd, sd, row, picked)
                 lst.append(keep.tile([P, S], F32, name="%s%d" % (name, t)))
                 nc.scalar.activation(out=lst[t][:], in_=bank[:], func=ACT.Copy, scale=gain[:, t : t + 1])
@@ -151,7 +150,7 @@ def tile_picked_hermite2_none_po_kernel(
 
         def terms(lo, hi, t, zt):
             entries = slice(lo // 16, hi // 16)
-            looked = ((y[t], k1_l, sm[t]), (c[t], k0_l, u1[t]), (c[t], k1_l, w[t]), (y[t], k0_l, h00[t]))
+            looked = ((c[t], k0_l, u1[t]), (c[t], k1_l, w[t]), (y[t], k1_l, sm[t]), (y[t], k0_l, h00[t]))
             for q, (window, lst, coef) in enumerate(looked):
                 term = ring.tile([P, hi - lo], F32, name="term", tag="term", bufs=12)
                 nc.vector.tensor_tensor(term[:], window[:].indirect(lst[:, entries]), coef[:, lo:hi], ALU.mult)
@@ -178,7 +177,7 @@ def tile_picked_hermite2_none_po_kernel(
             cols = slice(j0, j0 + BLK)
             rows = slice(t * P, (t + 1) * P)
             nc.tensor.matmul_mx(
-                out=out, lhsT=w4d[:, rows].bitcast(FP8X4), lhsT_scale=s4d[:, rows],
+                out=out, lhsT=w4d[:, rows].bitcast(FP8X4), lhsT_scale=s24d[4:P, rows],
                 rhs=z_codes[:, cols].bitcast(FP8X4), rhs_scale=z_scales[:, cols], start=True, stop=True,
             )
 

from contextlib import ExitStack

import concourse.mybir as mybir
from concourse.masks import make_identity

K, T, S, N, H = 512, 2048, 512, 512, 512
FLOPS = 2 * (3 * K * H * S + H * N * S)

F32 = mybir.dt.float32
BF16 = mybir.dt.bfloat16
I32 = mybir.dt.int32
U32 = mybir.dt.uint32
U16 = mybir.dt.uint16
U8 = mybir.dt.uint8
FP8X4 = mybir.dt.float8_e4m3fn_x4
ACT = mybir.ActivationFunctionType
ALU = mybir.AluOpType

P = 128
PACK = 4
QUADS = 4
BLK = 128
PIECES = ((0, 256), (256, 384), (384, 512))


def tile_picked_hermite2_none_po_kernel(
    tc, x_words, x_scales, w1_words, w1_scales, w2_words, w2_scales, w3_words, w3_scales, gn,
    w4_words, w4_scales, offs, two, thr, k0, k1, out_0, out_1, out_2,
):
    nc = tc.nc
    with ExitStack() as ctx:
        keep = ctx.enter_context(tc.tile_pool(name="keep", bufs=1))
        ring = ctx.enter_context(tc.tile_pool(name="ring", bufs=2))
        psum = ctx.enter_context(tc.psum_pool(name="psum", bufs=1))

        def load_list(name, src):
            tile = keep.tile([P, S // 16], U16, name=name)
            nc.sync.dma_start(tile[:], src)
            return tile

        def load_words(name, src, width):
            tile = keep.tile([P, width], I32, name=name, tag=name, align_bytes=64)
            nc.sync.dma_start(tile[:], src[0].rearrange("p n t -> p (n t)").bitcast(I32))
            return tile

        def load_scale_rows(queue, tile, src, row):
            for q in range(QUADS):
                queue.dma_start(
                    tile[32 * q + row : 32 * q + row + 4, :].bitcast(I32),
                    src[0, 4 * q : 4 * q + 4, :].bitcast(I32),
                )

        def zeroed_bytes(engine, name, width):
            tile = keep.tile([P, width], U8, name=name, tag=name, align_bytes=64)
            engine.memset(tile[:].bitcast(I32), 0)
            return tile

        def deal(name, tile, dtype, run, slot=None):
            dealt = keep.tile([P, H], dtype, name=name, tag=slot or name, align_bytes=64)
            nc.vector.tensor_copy(
                out=dealt[:].rearrange("p (t c i) -> p c t i", t=PACK, i=run),
                in_=tile[:].rearrange("p (c i t) -> p c t i", t=PACK, i=run),
            )
            return dealt

        xs = zeroed_bytes(nc.vector, "xs", T)
        s31 = zeroed_bytes(nc.vector, "s31", H)
        s24 = zeroed_bytes(nc.gpsimd, "s24", H)

        w3 = load_words("w3", w3_words, H)
        load_scale_rows(nc.sync, xs, x_scales, 0)
        thr_l = load_list("thr_l", thr)
        offs_l = load_list("offs_l", offs)
        xw = load_words("xw", x_words, T)
        two_l = load_list("two_l", two)
        w1 = load_words("w1", w1_words, H)
        w2 = load_words("w2", w2_words, H)
        k0_l = load_list("k0_l", k0)
        k1_l = load_list("k1_l", k1)
        gain = keep.tile([P, PACK], F32, name="gain")
        nc.sync.dma_start(gain[:], gn.rearrange("(p t) o -> p (t o)", t=PACK))
        load_scale_rows(nc.sync, s31, w3_scales, 0)
        load_scale_rows(nc.sync, s31, w1_scales, 4)
        w4 = load_words("w4", w4_words, N)
        load_scale_rows(nc.gpsimd, s24, w2_scales, 0)
        load_scale_rows(nc.gpsimd, s24, w4_scales, 4)
        ident = keep.tile([P, P], F32, name="ident")
        make_identity(nc, ident[:])

        def pick_words(name, lst, slot):
            words = keep.tile([P, S], U32, name=name, tag=slot, align_bytes=64)
            nc.vector.tensor_copy(words[:], xw[:].bitcast(U32).indirect(lst[:]))
            return words

        def pick_scales(name, lst, slot):
            scales = keep.tile([P, S], U8, name=name, tag=slot, align_bytes=64)
            nc.vector.tensor_copy(scales[:], xs[:].indirect(lst[:]))
            return scales

        def project(t, wd, sd, row, picked):
            bank = psum.tile([P, S], F32, name="mm", tag="mm", bufs=3)
            cols = slice(t * P, (t + 1) * P)
            nc.tensor.matmul_mx(
                out=bank[:], lhsT=wd[:, cols].bitcast(FP8X4), lhsT_scale=sd[row:P, cols],
                rhs=picked[0][:].bitcast(FP8X4), rhs_scale=picked[1][:], start=True, stop=True,
            )
            return bank

        w3d = deal("w3d", w3, I32, 4)
        thr_s = pick_scales("thr_s", thr_l, "thr_s")
        offs_s = pick_scales("offs_s", offs_l, "offs_s")
        x_thr = (pick_words("thr_w", thr_l, "thr_w"), thr_s)
        two_s = pick_scales("two_s", two_l, "two_s")
        x_offs = (pick_words("offs_w", offs_l, "offs_w"), offs_s)
        s31d = deal("s31d", s31, U8, 16)
        x_two = (pick_words("two_w", two_l, "s31"), two_s)
        w1d = deal("w1d", w1, I32, 4)
        w2d = deal("w2d", w2, I32, 4)
        s24d = deal("s24d", s24, U8, 16, "xw")
        w4d = deal("w4d", w4, I32, 4)
        d, d2, e2 = [], [], []

        def positions(t):
            bank = project(t, w3d, s31d, 0, x_thr)
            for lst, name in ((d, "d"), (d2, "d2_"), (e2, "e2_")):
                lst.append(keep.tile([P, S], F32, name="%s%d" % (name, t)))
            nc.scalar.activation(out=d[t][:], in_=bank[:], func=ACT.Sigmoid)
            nc.scalar.activation(out=d2[t][:], in_=d[t][:], func=ACT.Square)
            nc.scalar.activation(out=e2[t][:], in_=d[t][:], func=ACT.Square, scale=-1.0, bias=1.0)

        z_scales = keep.tile([P, S], U8, name="z_scales", align_bytes=64)
        z_codes = keep.tile([P, S], U32, name="z_codes", align_bytes=64)
        o_scales = keep.tile([P, S], U8, name="o_scales", align_bytes=64)
        o_codes = keep.tile([P, S], I32, name="o_codes", align_bytes=64)
        y, c, h00, sm, u1, w = [], [], [], [], [], []

        def windows(t):
            for lst, wd, sd, row, picked, name in ((y, w1d, s31d, 4, x_offs, "y"), (c, w2d, s24d, 0, x_two, "c")):
                bank = project(t, wd, sd, row, picked)
                lst.append(keep.tile([P, S], F32, name="%s%d" % (name, t)))
                nc.scalar.activation(out=lst[t][:], in_=bank[:], func=ACT.Copy, scale=gain[:, t : t + 1])

        def coefficients(t):
            for lst, name in ((h00, "h00_"), (sm, "sm"), (u1, "u1_"), (w, "w_")):
                lst.append(keep.tile([P, S], F32, name="%s%d" % (name, t)))
            nc.vector.scalar_tensor_tensor(out=w[t][:], in0=d[t][:], scalar=-1.0, in1=d2[t][:], op0=ALU.add, op1=ALU.mult)
            nc.vector.tensor_tensor(out=u1[t][:], in0=d[t][:], in1=e2[t][:], op=ALU.mult)
            nc.vector.scalar_tensor_tensor(out=sm[t][:], in0=w[t][:], scalar=-2.0, in1=d2[t][:], op0=ALU.mult, op1=ALU.add)
            nc.scalar.activation(out=h00[t][:], in_=sm[t][:], func=ACT.Identity, scale=-1.0, bias=1.0)

        def terms(lo, hi, t, zt):
            entries = slice(lo // 16, hi // 16)
            looked = ((c[t], k0_l, u1[t]), (c[t], k1_l, w[t]), (y[t], k1_l, sm[t]), (y[t], k0_l, h00[t]))
            for q, (window, lst, coef) in enumerate(looked):
                term = ring.tile([P, hi - lo], F32, name="term", tag="term", bufs=12)
                nc.vector.tensor_tensor(term[:], window[:].indirect(lst[:, entries]), coef[:, lo:hi], ALU.mult)
                for b in range((hi - lo) // BLK):
                    nc.tensor.matmul(
                        out=zt[b][:, t % 2, :], lhsT=term[:, b * BLK : (b + 1) * BLK], rhs=ident[:],
                        is_transpose=True, start=(q == 0), stop=(q == len(looked) - 1),
                    )

        def turn_back(u, zt, back):
            pairs = ring.tile([P, P, 2], BF16, name="pairs", tag="pairs", bufs=3)
            nc.scalar.copy(out=pairs[:], in_=zt[:].rearrange("j e p -> j p e"))
            nc.tensor.transpose(back[:, u, :], pairs[:].rearrange("j p e -> j (p e)").bitcast(F32), ident[:])

        def quantize_z(j0, back):
            grouped = ring.tile([P, BLK * PACK], BF16, name="grouped", tag="grouped", bufs=2, align_bytes=64)
            nc.scalar.copy(
                out=grouped[:].bitcast(F32).rearrange("p (j u) -> p j u", u=2), in_=back[:].rearrange("p u j -> p j u")
            )
            cols = slice(j0, j0 + BLK)
            nc.vector.quantize_mx(out=z_codes[:, cols].bitcast(FP8X4), scales=z_scales[:, cols], in_=grouped[:])

        def last_product(j0, t, out):
            cols = slice(j0, j0 + BLK)
            rows = slice(t * P, (t + 1) * P)
            nc.tensor.matmul_mx(
                out=out, lhsT=w4d[:, rows].bitcast(FP8X4), lhsT_scale=s24d[4:P, rows],
                rhs=z_codes[:, cols].bitcast(FP8X4), rhs_scale=z_scales[:, cols], start=True, stop=True,
            )

        out_rows = out_0.rearrange("(p t) j -> p t j", t=PACK)

        def layer(j0):
            bank = psum.tile([P, PACK, BLK], F32, name="mm", tag="mm", bufs=3)
            for t in range(PACK):
                last_product(j0, t, bank[:, t, :])
            rounded = ring.tile([P, BLK * PACK], BF16, name="rounded", tag="rounded", bufs=2, align_bytes=64)
            nc.scalar.copy(out=rounded[:].rearrange("p (j t) -> p j t", t=PACK), in_=bank[:].rearrange("p t j -> p j t"))
            result = ring.tile([P, PACK, BLK], F32, name="result", tag="result", bufs=4)
            nc.scalar.copy(out=result[:], in_=bank[:])
            nc.sync.dma_start(out_rows[:, :, j0 : j0 + BLK], result[:])
            return rounded

        def last_layer(j0):
            result = ring.tile([P, PACK, BLK], F32, name="result", tag="result", bufs=4)
            for u, copy in enumerate((nc.scalar.copy, nc.vector.tensor_copy)):
                bank = psum.tile([P, 2, BLK], F32, name="mm", tag="mm", bufs=3)
                for e in range(2):
                    last_product(j0, 2 * u + e, bank[:, e, :])
                copy(out=result[:, 2 * u : 2 * u + 2, :], in_=bank[:])
            nc.scalar.dma_start(out_rows[:, :, j0 : j0 + BLK], result[:])
            rounded = ring.tile([P, BLK * PACK], BF16, name="rounded", tag="rounded", bufs=2, align_bytes=64)
            nc.vector.tensor_copy(
                out=rounded[:].rearrange("p (c i t) -> p c t i", t=PACK, i=4),
                in_=result[:].rearrange("p t (c i) -> p c t i", i=4),
            )
            return rounded

        def quantize_out(j0, rounded):
            cols = slice(j0, j0 + BLK)
            nc.vector.quantize_mx(out=o_codes[:, cols].bitcast(FP8X4), scales=o_scales[:, cols], in_=rounded[:])
            nc.sync.dma_start(out_1[0].rearrange("p n t -> p (n t)").bitcast(I32)[:, cols], o_codes[:, cols])

        pending = []
        for lo, hi in PIECES:
            blocks = range(lo, hi, BLK)
            back = [psum.tile([P, 2, BLK], F32, name="back", tag="back", bufs=2) for j0 in blocks]
            for t in range(PACK):
                if lo == 0:
                    positions(t)
                    windows(t)
                    coefficients(t)
                if t % 2 == 0:
                    zt = [psum.tile([P, 2, P], F32, name="zt", tag="zt", bufs=3) for j0 in blocks]
                terms(lo, hi, t, zt)
                if t == 0:
                    for j0, old in pending:
                        quantize_z(j0, old)
                if t == 1:
                    pending = [(j0, layer(j0)) for j0, old in pending]
                if t == 2:
                    for j0, rounded in pending:
                        quantize_out(j0, rounded)
                if t % 2 == 1:
                    for b in range(len(blocks)):
                        turn_back(t // 2, zt[b], back[b])
            pending = list(zip(blocks, back))
        for j0, old in pending:
            quantize_z(j0, old)
            quantize_out(j0, last_layer(j0))
        for q in range(QUADS):
            queue = nc.scalar if q % 2 else nc.sync
            queue.dma_start(
                out_2[0, 4 * q : 4 * q + 4, :].bitcast(I32), o_scales[32 * q : 32 * q + 4, :].bitcast(I32)
            )
